import numpy as np, ml_dtypes
CORES = [4,44,84,124]
N = 4
ROOT = 2
def setup_inputs(rng):
    return {"x": rng.standard_normal((N, 128, N * 512), dtype=np.float32).astype(ml_dtypes.bfloat16)}
def reference(x):
    return {"y": np.stack([x[ROOT][:, r * 512:(r + 1) * 512] for r in range(N)])}

@@ -1,0 +1,55 @@
+W = 512
+
+SCRATCH = {
+    "stage": ("dram", [3, 128, W], "bfloat16"),
+    "land": ("dram", [128, W], "bfloat16"),
+}
+SEMAPHORES = ["ld0", "ld1", "ld2", "own", "sent", "arrived", "stored"]
+
+
+def rank_program(g, core, T, topo):
+    root = T.cores[T.root]
+    chip0 = topo.chip(root) * 8
+    ports = [chip0 + 6, chip0 + 2]
+    via = {}
+    for r, c in enumerate(T.cores):
+        if c == root:
+            continue
+        if topo.may_write(root, c):
+            via[r] = None
+        else:
+            via[r] = ports[len([v for v in via.values() if v is not None]) % 2]
+    order = sorted(via, key=lambda r: via[r] is None)
+
+    def send(dst, src_ap):
+        rid, pid, _se = topo.addr(dst)
+        m = topo.mask(core, dst)
+        g.remote_dma(T.land[:], src_ap, T.sem.arrived, T.sem.sent, pid, rid, m)
+        return 16 if m == 0xFFFF else 8
+
+    if core == root:
+        q = [g.sync, g.scalar]
+        for i, r in enumerate(order):
+            q[i % 2].dma_start(T.stage[i], T.x[:, r * W:(r + 1) * W]).then_inc(T.sem["ld%d" % i], 16)
+        q[len(order) % 2].dma_start(T.y[:], T.x[:, T.root * W:(T.root + 1) * W]).then_inc(T.sem.own, 16)
+        left = 0
+        for i, r in enumerate(order):
+            g.wait_ge(T.sem["ld%d" % i], 16)
+            left += send(T.cores[r] if via[r] is None else via[r], T.stage[i])
+        g.wait_ge(T.sem.sent, left)
+        g.wait_ge(T.sem.own, 16)
+        return
+
+    for r, v in via.items():
+        if core == v:
+            g.wait_ge(T.sem.arrived, 16)
+            n = send(T.cores[r], T.land[:])
+            g.wait_ge(T.sem.sent, n)
+            return
+
+    rank = T.rank_of(core)
+    if rank is None:
+        return
+    g.sync.wait_ge(T.sem.arrived, 8)
+    g.sync.dma_start(T.y[:], T.land[:]).then_inc(T.sem.stored, 16)
+    g.wait_ge(T.sem.stored, 16)

@@ -1,55 +1,68 @@
 W = 512
+RA = 32
+LO, HI = 0x00FF, 0xFF00
 
 SCRATCH = {
-    "stage": ("dram", [3, 128, W], "bfloat16"),
-    "land": ("dram", [128, W], "bfloat16"),
+    "stageA": ("dram", [3, 128, RA * W // 128], "bfloat16"),
+    "stageB": ("dram", [3, 128, (128 - RA) * W // 128], "bfloat16"),
+    "landA": ("dram", [128, RA * W // 128], "bfloat16"),
+    "landB": ("dram", [128, (128 - RA) * W // 128], "bfloat16"),
 }
-SEMAPHORES = ["ld0", "ld1", "ld2", "own", "sent", "arrived", "stored"]
+SEMAPHORES = ["ldA0", "ldA1", "ldA2", "ldB0", "ldB1", "ldB2", "own", "sent", "arrA", "arrB", "stored"]
+
+
+def plan(T, topo):
+    root = T.cores[T.root]
+    home = topo.chip(root) * 8
+    mate_ports = [home + 6, home + 2]
+    big, small = [], []
+    for r, c in enumerate(T.cores):
+        if c == root:
+            continue
+        slot = len(small)
+        if topo.may_write(root, c):
+            big.append(("B", slot, r, home + 0))
+            small.append(("A", slot, r, None))
+        else:
+            big.insert(0, ("B", slot, r, mate_ports.pop(0)))
+            small.insert(0, ("A", slot, r, (topo.chip(c) ^ 1) * 8 + 6))
+    engines = [HI, LO, HI]
+    return [p + (engines[i],) for i, p in enumerate(big)] + [p + (LO,) for p in small]
 
 
 def rank_program(g, core, T, topo):
     root = T.cores[T.root]
-    chip0 = topo.chip(root) * 8
-    ports = [chip0 + 6, chip0 + 2]
-    via = {}
-    for r, c in enumerate(T.cores):
-        if c == root:
-            continue
-        if topo.may_write(root, c):
-            via[r] = None
-        else:
-            via[r] = ports[len([v for v in via.values() if v is not None]) % 2]
-    order = sorted(via, key=lambda r: via[r] is None)
+    steps = plan(T, topo)
 
-    def send(dst, src_ap):
+    def send(piece, dst, src_ap, engines):
         rid, pid, _se = topo.addr(dst)
-        m = topo.mask(core, dst)
-        g.remote_dma(T.land[:], src_ap, T.sem.arrived, T.sem.sent, pid, rid, m)
-        return 16 if m == 0xFFFF else 8
+        g.remote_dma(T["land" + piece][:], src_ap, T.sem["arr" + piece], T.sem.sent, pid, rid, engines)
 
     if core == root:
         q = [g.sync, g.scalar]
-        for i, r in enumerate(order):
-            q[i % 2].dma_start(T.stage[i], T.x[:, r * W:(r + 1) * W]).then_inc(T.sem["ld%d" % i], 16)
-        q[len(order) % 2].dma_start(T.y[:], T.x[:, T.root * W:(T.root + 1) * W]).then_inc(T.sem.own, 16)
-        left = 0
-        for i, r in enumerate(order):
-            g.wait_ge(T.sem["ld%d" % i], 16)
-            left += send(T.cores[r] if via[r] is None else via[r], T.stage[i])
-        g.wait_ge(T.sem.sent, left)
+        for i, (piece, slot, r, _relay, _m) in enumerate(steps):
+            rows = slice(0, RA) if piece == "A" else slice(RA, 128)
+            q[i % 2].dma_start(T["stage" + piece][slot], T.x[rows, r * W:(r + 1) * W]).then_inc(
+                T.sem["ld%s%d" % (piece, slot)], 16)
+        q[len(steps) % 2].dma_start(T.y[:], T.x[:, T.root * W:(T.root + 1) * W]).then_inc(T.sem.own, 16)
+        for piece, slot, r, relay, m in steps:
+            g.wait_ge(T.sem["ld%s%d" % (piece, slot)], 16)
+            send(piece, T.cores[r] if relay is None else relay, T["stage" + piece][slot], m)
+        g.wait_ge(T.sem.sent, 8 * len(steps))
         g.wait_ge(T.sem.own, 16)
         return
 
-    for r, v in via.items():
-        if core == v:
-            g.wait_ge(T.sem.arrived, 16)
-            n = send(T.cores[r], T.land[:])
-            g.wait_ge(T.sem.sent, n)
+    for piece, _slot, r, relay, _m in steps:
+        if core == relay:
+            g.wait_ge(T.sem["arr" + piece], 8)
+            send(piece, T.cores[r], T["land" + piece][:], LO)
+            g.wait_ge(T.sem.sent, 8)
             return
 
-    rank = T.rank_of(core)
-    if rank is None:
+    if T.rank_of(core) is None:
         return
-    g.sync.wait_ge(T.sem.arrived, 8)
-    g.sync.dma_start(T.y[:], T.land[:]).then_inc(T.sem.stored, 16)
-    g.wait_ge(T.sem.stored, 16)
+    g.sync.wait_ge(T.sem.arrA, 8)
+    g.sync.dma_start(T.y[0:RA, :], T.landA[:]).then_inc(T.sem.stored, 16)
+    g.scalar.wait_ge(T.sem.arrB, 8)
+    g.scalar.dma_start(T.y[RA:128, :], T.landB[:]).then_inc(T.sem.stored, 16)
+    g.wait_ge(T.sem.stored, 32)

W = 512
RA = 32
LO, HI = 0x00FF, 0xFF00

SCRATCH = {
    "stageA": ("dram", [3, 128, RA * W // 128], "bfloat16"),
    "stageB": ("dram", [3, 128, (128 - RA) * W // 128], "bfloat16"),
    "landA": ("dram", [128, RA * W // 128], "bfloat16"),
    "landB": ("dram", [128, (128 - RA) * W // 128], "bfloat16"),
}
SEMAPHORES = ["ldA0", "ldA1", "ldA2", "ldB0", "ldB1", "ldB2", "own", "sent", "arrA", "arrB", "stored"]


def plan(T, topo):
    root = T.cores[T.root]
    home = topo.chip(root) * 8
    mate_ports = [home + 6, home + 2]
    big, small = [], []
    for r, c in enumerate(T.cores):
        if c == root:
            continue
        slot = len(small)
        if topo.may_write(root, c):
            big.append(("B", slot, r, home + 0))
            small.append(("A", slot, r, None))
        else:
            big.insert(0, ("B", slot, r, mate_ports.pop(0)))
            small.insert(0, ("A", slot, r, (topo.chip(c) ^ 1) * 8 + 6))
    engines = [HI, LO, HI]
    return [p + (engines[i],) for i, p in enumerate(big)] + [p + (LO,) for p in small]


def rank_program(g, core, T, topo):
    root = T.cores[T.root]
    steps = plan(T, topo)

    def send(piece, dst, src_ap, engines):
        rid, pid, _se = topo.addr(dst)
        g.remote_dma(T["land" + piece][:], src_ap, T.sem["arr" + piece], T.sem.sent, pid, rid, engines)

    if core == root:
        q = [g.sync, g.scalar]
        for i, (piece, slot, r, _relay, _m) in enumerate(steps):
            rows = slice(0, RA) if piece == "A" else slice(RA, 128)
            q[i % 2].dma_start(T["stage" + piece][slot], T.x[rows, r * W:(r + 1) * W]).then_inc(
                T.sem["ld%s%d" % (piece, slot)], 16)
        q[len(steps) % 2].dma_start(T.y[:], T.x[:, T.root * W:(T.root + 1) * W]).then_inc(T.sem.own, 16)
        for piece, slot, r, relay, m in steps:
            g.wait_ge(T.sem["ld%s%d" % (piece, slot)], 16)
            send(piece, T.cores[r] if relay is None else relay, T["stage" + piece][slot], m)
        g.wait_ge(T.sem.sent, 8 * len(steps))
        g.wait_ge(T.sem.own, 16)
        return

    for piece, _slot, r, relay, _m in steps:
        if core == relay:
            g.wait_ge(T.sem["arr" + piece], 8)
            send(piece, T.cores[r], T["land" + piece][:], LO)
            g.wait_ge(T.sem.sent, 8)
            return

    if T.rank_of(core) is None:
        return
    g.sync.wait_ge(T.sem.arrA, 8)
    g.sync.dma_start(T.y[0:RA, :], T.landA[:]).then_inc(T.sem.stored, 16)
    g.scalar.wait_ge(T.sem.arrB, 8)
    g.scalar.dma_start(T.y[RA:128, :], T.landB[:]).then_inc(T.sem.stored, 16)
    g.wait_ge(T.sem.stored, 32)
